import numpy as np
import ml_dtypes


def mxq(x, axis, fmt="e4m3"):
    dtype, down = {"e4m3": (ml_dtypes.float8_e4m3fn, 7), "e5m2": (ml_dtypes.float8_e5m2, 14)}[fmt]
    v = np.moveaxis(np.asarray(x, np.float32).astype(ml_dtypes.bfloat16).astype(np.float64), axis, -1)
    blocks = v.reshape(v.shape[:-1] + (-1, 32))
    amax = np.abs(blocks).max(-1, keepdims=True)
    byte = np.maximum(np.where(amax > 0, np.frexp(amax)[1] - 1 + 127, 0) - down, 1)
    scale = np.exp2(byte - 127.0)
    codes = (blocks / scale).astype(np.float32).astype(dtype).astype(np.float64)
    return np.moveaxis((codes * scale).reshape(v.shape), -1, axis)


WIDE = False


def mx_kscale(k):
    if not WIDE:
        return np.ones(k)
    levels = np.array([30, -30])
    if k % 512:
        return np.exp2(np.random.permutation(np.resize(levels, k // 32))).repeat(32)
    a = np.empty((k // 512, 16))
    for p in range(k // 512):
        a[p, :8] = np.random.permutation(np.resize(levels, 8))
        for g in range(8):
            far = levels[np.abs(levels - a[p, g]) >= 10]
            a[p, g + 8] = far[np.random.randint(len(far))]
    return np.exp2(a.ravel()).repeat(32)


BF16 = ml_dtypes.bfloat16


def bf(x):
    return np.asarray(x, np.float32).astype(BF16)


def f64(x):
    return np.asarray(x).astype(np.float64)


E2M1 = np.array([0.0, 0.5, 1.0, 1.5, 2.0, 3.0, 4.0, 6.0, -0.0, -0.5, -1.0, -1.5, -2.0, -3.0, -4.0, -6.0])


def pack_weight(w, fmt):
    k, n = w.shape
    w = f64(bf(w)).reshape(k // 32, 32, n)
    amax = np.abs(w).max(1)
    if fmt in ("e4m3", "e5m2"):
        byte = np.frexp(amax)[1] - 1 + 127 - (7 if fmt == "e4m3" else 14)
    else:
        mant, ex = np.frexp(amax / 6.0)
        byte = np.where(mant > 0.5, ex, ex - 1) + 127
    byte = np.clip(np.where(amax > 0, byte, 1), 1, 254)
    scaled = (w * np.exp2(127.0 - byte)[:, None, :]).reshape(k, n).astype(np.float32)
    by_word = np.ascontiguousarray(scaled.reshape(k // 512, 128, 4, n).transpose(0, 1, 3, 2))
    if fmt in ("e4m3", "e5m2"):
        words = by_word.astype(ml_dtypes.float8_e4m3fn if fmt == "e4m3" else ml_dtypes.float8_e5m2).view(np.uint8)
    else:
        c = by_word.astype(ml_dtypes.float4_e2m1fn).view(np.uint8) & 0xF
        words = c[..., 0::2] | (c[..., 1::2] << 4)
    return np.ascontiguousarray(words), np.ascontiguousarray(byte.astype(np.uint8).reshape(k // 512, 16, n))


def unpack_weight(words, scales, fmt):
    g, p, n, _ = words.shape
    if fmt in ("e4m3", "e5m2"):
        vals = np.ascontiguousarray(words).view(ml_dtypes.float8_e4m3fn if fmt == "e4m3" else ml_dtypes.float8_e5m2).astype(np.float64)
    else:
        nib = np.empty((g, p, n, 4), np.uint8)
        nib[..., 0::2] = words & 0xF
        nib[..., 1::2] = words >> 4
        vals = E2M1[nib]
    vals = vals * np.repeat(np.exp2(scales.astype(np.float64) - 127.0), 8, axis=1)[..., None]
    return vals.transpose(0, 1, 3, 2).reshape(g * 512, n)


K, S, B, P, F = 2048, 16, 1024, 1024, 512


def setup_inputs():
    s = mx_kscale(K)
    t = mx_kscale(P)
    y = np.random.standard_normal((K, B)) * np.exp(0.5 * np.random.standard_normal((K, B)))
    y_words, y_scales = pack_weight(y * s[:, None], "e5m2")
    w = np.random.standard_normal((P, K // S, S)) / np.sqrt(K)
    w = (w - w.mean(axis=2, keepdims=True)).reshape(P, K)
    return {"y_words": y_words,
            "y_scales": y_scales,
            "w": bf(w / s * t[:, None]),
            "sens": bf(np.exp(0.4 * np.random.standard_normal((P, B)))),
            "d": bf(np.random.standard_normal((P, F)) / np.sqrt(P) / t[:, None]),
            "tau": bf(0.3 + 0.1 * np.abs(np.random.standard_normal(F)))}


def reference(y_words, y_scales, w, sens, d, tau):
    y = unpack_weight(y_words, y_scales, "e5m2")
    r = mxq(f64(w), 1, "e4m3") @ y
    z = r * f64(sens)
    score = mxq(f64(d), 0, "e4m3").T @ mxq(z, 0, "e5m2")
    return np.maximum(np.abs(score) - f64(tau)[:, None], 0.0)

@@ -1,0 +1,278 @@
+from contextlib import ExitStack
+
+import concourse.mybir as mybir
+from concourse.masks import make_identity
+
+K, B, PR, F = 2048, 1024, 1024, 512
+FLOPS = 2 * PR * K * B + 2 * F * PR * B
+
+F32 = mybir.dt.float32
+BF16 = mybir.dt.bfloat16
+I32 = mybir.dt.int32
+U32 = mybir.dt.uint32
+U8 = mybir.dt.uint8
+E4 = mybir.dt.float8_e4m3fn_x4
+E5 = mybir.dt.float8_e5m2_x4
+ALU = mybir.AluOpType
+ACT = mybir.ActivationFunctionType
+
+P = 128
+PACK = 4
+N = 512
+G = K // 512
+BANKS = 8
+
+
+def tile_parity_fault_isolation_e3_kernel(tc, y_words, y_scales, w, sens, d, tau, out):
+    nc = tc.nc
+    with ExitStack() as ctx:
+        sb = ctx.enter_context(tc.tile_pool(name="sb", bufs=1))
+        ps = ctx.enter_context(tc.psum_pool(name="ps", bufs=1))
+        ctx.enter_context(tc.manual_schedule())
+
+        def sbuf(name, shape, dtype):
+            return sb.tile(shape, dtype, name=name, align_bytes=64)
+
+        banks_taken = []
+
+        def next_bank():
+            n = len(banks_taken)
+            bank = ps.tile([P, N], F32, name="bank%d" % n, tag="bank%d" % (n % BANKS))
+            banks_taken.append(bank)
+            return bank
+
+        ident = sbuf("ident", [P, P], F32)
+        warm = sbuf("warm", [P, 1], F32)
+        warm_out = sbuf("warm_out", [P, 1], F32)
+        w_rows = [sbuf("w_rows%d" % i, [P, K], BF16) for i in range(8)]
+        w_t = [sbuf("w_t%d" % i, [P, G, P, PACK], BF16) for i in range(8)]
+        w_codes = [sbuf("w_codes%d" % i, [P, G * P], U32) for i in range(8)]
+        w_scale = [sbuf("w_scale%d" % i, [P, G * P], U8) for i in range(8)]
+        y_codes = [sbuf("y_codes%d" % c, [P, G, N], U32) for c in range(2)]
+        y_scale = [sbuf("y_scale%d" % c, [P, G, N], U8) for c in range(2)]
+        hc = [(h, c) for h in range(2) for c in range(2)]
+        s_sb = {(h, c): sbuf("s%d%d" % (h, c), [P, PACK, N], BF16) for h, c in hc}
+        z_rows = {(h, c): sbuf("z_rows%d%d" % (h, c), [P, PACK, N], BF16) for h, c in hc}
+        z_il = {(h, c): sbuf("z_il%d%d" % (h, c), [P, N, PACK], BF16) for h, c in hc}
+        z_codes = {(h, c): sbuf("z_codes%d%d" % (h, c), [P, N], U32) for h, c in hc}
+        z_scale = {(h, c): sbuf("z_scale%d%d" % (h, c), [P, N], U8) for h, c in hc}
+        d_rows = [sbuf("d_rows%d" % h, [P, PACK, F], BF16) for h in range(2)]
+        d_il = [sbuf("d_il%d" % h, [P, F, PACK], BF16) for h in range(2)]
+        d_codes = [sbuf("d_codes%d" % h, [P, F], U32) for h in range(2)]
+        d_scale = [sbuf("d_scale%d" % h, [P, F], U8) for h in range(2)]
+        tau_raw = sbuf("tau_raw", [P, 4, 2], BF16)
+        tau_sb = sbuf("tau_sb", [P, 4], F32)
+
+        t_banks = {}
+        r_bank = {}
+        o_bank = {}
+        mag = {}
+        res = {}
+
+        def cols(c):
+            return slice(c * N, (c + 1) * N)
+
+        def load_w(i, k0, k1):
+            h, t = divmod(i, PACK)
+            rows = w[h * 512:(h + 1) * 512, :].rearrange("(m t) k -> t m k", t=PACK)[t]
+            nc.sync.dma_start(out=w_rows[i][:, k0:k1], in_=rows[:, k0:k1])
+
+        def load_y_scale(c):
+            for q in range(4):
+                src = y_scales[:, 4 * q:4 * q + 4, cols(c)].rearrange("g r n -> r g n")
+                nc.sync.dma_start(out=y_scale[c][32 * q:32 * q + 4, :, :].bitcast(I32), in_=src.bitcast(I32))
+
+        def load_y(c, g0, g1):
+            src = y_words.rearrange("g p n t -> p g (n t)")[:, g0:g1, c * N * PACK:(c + 1) * N * PACK]
+            nc.sync.dma_start(out=y_codes[c][:, g0:g1, :].bitcast(I32), in_=src.bitcast(I32))
+
+        def load_sens(h, c):
+            src = sens[h * 512:(h + 1) * 512, cols(c)].rearrange("(p t) n -> p t n", t=PACK)
+            nc.sync.dma_start(out=s_sb[h, c][:], in_=src)
+
+        def load_d(h):
+            src = d[h * 512:(h + 1) * 512, :].rearrange("(p t) f -> p t f", t=PACK)
+            nc.sync.dma_start(out=d_rows[h][:], in_=src)
+
+        def load_tau():
+            with nc.allow_non_contiguous_dma(reason="one threshold to a partition"):
+                nc.sync.dma_start(out=tau_raw[:, :, 0], in_=tau.rearrange("(j p) -> p j", p=P))
+
+        def transpose_w(i, half):
+            bank = next_bank()
+            t_banks[i, half] = bank
+            words = w_rows[i][:].bitcast(F32)
+            for gl in range(2):
+                g = 2 * half + gl
+                for u in range(2):
+                    slot = 2 * gl + u
+                    nc.tensor.transpose(bank[:, slot * P:(slot + 1) * P],
+                                        words[:, 256 * g + u:256 * (g + 1):2], ident[:])
+
+        def copy_w(i, half):
+            dst = w_t[i][:, 2 * half:2 * half + 2, :, :].bitcast(F32)
+            nc.scalar.copy(out=dst, in_=t_banks[i, half][:].rearrange("p (g u m) -> p g m u", g=2, u=2))
+
+        def quant_w(i, g0, g1):
+            nc.vector.quantize_mx(out=w_codes[i][:, g0 * P:g1 * P].bitcast(E4),
+                                  scales=w_scale[i][:, g0 * P:g1 * P],
+                                  in_=w_t[i][:, g0:g1, :, :].rearrange("p g m t -> p (g m t)"))
+
+        def stage1(i, c):
+            bank = next_bank()
+            r_bank[i, c] = bank
+            for g in range(G):
+                nc.tensor.matmul_mx(out=bank[:],
+                                    lhsT=w_codes[i][:, g * P:(g + 1) * P].bitcast(E4),
+                                    lhsT_scale=w_scale[i][:, g * P:(g + 1) * P],
+                                    rhs=y_codes[c][:, g, :].bitcast(E5),
+                                    rhs_scale=y_scale[c][:, g, :],
+                                    start=(g == 0), stop=(g == G - 1))
+
+        def weigh(i, c):
+            h, t = divmod(i, PACK)
+            nc.vector.tensor_tensor(out=z_rows[h, c][:, t, :], in0=r_bank[i, c][:], in1=s_sb[h, c][:, t, :],
+                                    op=ALU.mult)
+
+        def interleave(copy, dst, src):
+            copy(out=dst[:].rearrange("p (n i) t -> p n t i", i=4),
+                 in_=src[:].rearrange("p t (n i) -> p n t i", i=4))
+
+        def quant_z(h, c):
+            nc.vector.quantize_mx(out=z_codes[h, c][:].bitcast(E5), scales=z_scale[h, c][:],
+                                  in_=z_il[h, c][:].rearrange("p n t -> p (n t)"))
+
+        def quant_d(h):
+            nc.vector.quantize_mx(out=d_codes[h][:].bitcast(E4), scales=d_scale[h][:],
+                                  in_=d_il[h][:].rearrange("p f t -> p (f t)"))
+
+        def stage2(c, j, h):
+            if h == 0:
+                o_bank[c, j] = next_bank()
+            nc.tensor.matmul_mx(out=o_bank[c, j][:],
+                                lhsT=d_codes[h][:, j * P:(j + 1) * P].bitcast(E4),
+                                lhsT_scale=d_scale[h][:, j * P:(j + 1) * P],
+                                rhs=z_codes[h, c][:].bitcast(E5),
+                                rhs_scale=z_scale[h, c][:],
+                                start=(h == 0), stop=(h == 1))
+
+        def magnitude(c, j):
+            mag[c, j] = sbuf("mag%d%d" % (c, j), [P, N], F32)
+            nc.scalar.activation(out=mag[c, j][:], in_=o_bank[c, j][:], func=ACT.Abs)
+
+        def threshold(c, j):
+            res[c, j] = sbuf("res%d%d" % (c, j), [P, N], F32)
+            nc.vector.tensor_scalar(out=res[c, j][:], in0=mag[c, j][:], scalar1=tau_sb[:, j:j + 1], scalar2=0.0,
+                                    op0=ALU.subtract, op1=ALU.max)
+            nc.sync.dma_start(out=out[j * P:(j + 1) * P, cols(c)], in_=res[c, j][:])
+
+        def turn(i):
+            for half in range(2):
+                transpose_w(i, half)
+                copy_w(i, half)
+
+        v_copy = nc.vector.tensor_copy
+        s_copy = nc.scalar.copy
+
+        make_identity(nc, ident[:])
+        nc.vector.memset(warm[:], 0.0)
+        nc.scalar.activation(out=warm_out[:], in_=warm[:], func=ACT.Abs)
+        for c in range(2):
+            nc.vector.memset(y_scale[c][:].rearrange("p g n -> p (g n)").bitcast(I32), 0)
+
+        load_w(0, 0, K // 2)
+        load_w(0, K // 2, K)
+        load_w(1, 0, K)
+        load_y_scale(0)
+        load_y(0, 0, 2)
+        load_y(0, 2, 4)
+        load_w(2, 0, K)
+        load_w(3, 0, K)
+        load_sens(0, 0)
+        load_w(4, 0, K)
+        load_w(5, 0, K)
+        load_d(0)
+        load_w(6, 0, K)
+        load_w(7, 0, K)
+        load_sens(1, 0)
+        load_d(1)
+        load_y_scale(1)
+        load_y(1, 0, 2)
+        load_y(1, 2, 4)
+        load_sens(0, 1)
+        load_tau()
+        load_sens(1, 1)
+
+        turn(0)
+        quant_w(0, 0, 2)
+        quant_w(0, 2, 4)
+        turn(1)
+        quant_w(1, 0, G)
+        stage1(0, 0)
+        turn(2)
+        turn(3)
+        quant_w(2, 0, G)
+        stage1(1, 0)
+        weigh(0, 0)
+        quant_w(3, 0, G)
+        stage1(2, 0)
+        weigh(1, 0)
+        weigh(2, 0)
+        turn(4)
+        turn(5)
+        quant_w(4, 0, G)
+        quant_w(5, 0, G)
+        interleave(s_copy, d_il[0], d_rows[0])
+        stage1(3, 0)
+        weigh(3, 0)
+        stage1(4, 0)
+        weigh(4, 0)
+        interleave(v_copy, z_il[0, 0], z_rows[0, 0])
+        turn(6)
+        turn(7)
+        quant_d(0)
+        quant_w(6, 0, G)
+        quant_z(0, 0)
+        quant_w(7, 0, G)
+        interleave(s_copy, d_il[1], d_rows[1])
+        for i in (5, 6, 7):
+            stage1(i, 0)
+            weigh(i, 0)
+        interleave(s_copy, z_il[1, 0], z_rows[1, 0])
+        quant_d(1)
+        nc.vector.tensor_copy(out=tau_sb[:], in_=tau_raw[:, :, 0])
+        for i in (0, 1, 2):
+            stage1(i, 1)
+            weigh(i, 1)
+        quant_z(1, 0)
+        stage1(3, 1)
+        weigh(3, 1)
+        stage2(0, 0, 0)
+        stage2(0, 0, 1)
+        magnitude(0, 0)
+        interleave(s_copy, z_il[0, 1], z_rows[0, 1])
+        stage1(4, 1)
+        threshold(0, 0)
+        weigh(4, 1)
+        stage1(5, 1)
+        weigh(5, 1)
+        stage1(6, 1)
+        weigh(6, 1)
+        quant_z(0, 1)
+        stage1(7, 1)
+        weigh(7, 1)
+        interleave(v_copy, z_il[1, 1], z_rows[1, 1])
+        for j in (1, 2, 3):
+            stage2(0, j, 0)
+            stage2(0, j, 1)
+            magnitude(0, j)
+        threshold(0, 1)
+        quant_z(1, 1)
+        threshold(0, 2)
+        threshold(0, 3)
+        for j in range(4):
+            stage2(1, j, 0)
+        for j in range(4):
+            stage2(1, j, 1)
+            magnitude(1, j)
+            threshold(1, j)

@@ -45,6 +45,8 @@ def tile_parity_fault_isolation_e3_kernel(tc, y_words, y_scales, w, sens, d, tau
         warm = sbuf("warm", [P, 1], F32)
         warm_out = sbuf("warm_out", [P, 1], F32)
         w_rows = [sbuf("w_rows%d" % i, [P, K], BF16) for i in range(8)]
+        w_split = {}
+        idle = sbuf("idle", [P, 864], U32)
         w_t = [sbuf("w_t%d" % i, [P, G, P, PACK], BF16) for i in range(8)]
         w_codes = [sbuf("w_codes%d" % i, [P, G * P], U32) for i in range(8)]
         w_scale = [sbuf("w_scale%d" % i, [P, G * P], U8) for i in range(8)]
@@ -72,17 +74,18 @@ def tile_parity_fault_isolation_e3_kernel(tc, y_words, y_scales, w, sens, d, tau
         def cols(c):
             return slice(c * N, (c + 1) * N)
 
-        def load_w(i, k0, k1):
+        def load_w(i):
             h, t = divmod(i, PACK)
             rows = w[h * 512:(h + 1) * 512, :].rearrange("(m t) k -> t m k", t=PACK)[t]
-            nc.sync.dma_start(out=w_rows[i][:, k0:k1], in_=rows[:, k0:k1])
+            nc.sync.dma_start(out=w_rows[i][:], in_=rows)
 
         def load_y_scale(c):
             for q in range(4):
                 src = y_scales[:, 4 * q:4 * q + 4, cols(c)].rearrange("g r n -> r g n")
                 nc.sync.dma_start(out=y_scale[c][32 * q:32 * q + 4, :, :].bitcast(I32), in_=src.bitcast(I32))
 
-        def load_y(c, g0, g1):
+        def load_y(c, half):
+            g0, g1 = 2 * half, 2 * half + 2
             src = y_words.rearrange("g p n t -> p g (n t)")[:, g0:g1, c * N * PACK:(c + 1) * N * PACK]
             nc.sync.dma_start(out=y_codes[c][:, g0:g1, :].bitcast(I32), in_=src.bitcast(I32))
 
@@ -98,49 +101,69 @@ def tile_parity_fault_isolation_e3_kernel(tc, y_words, y_scales, w, sens, d, tau
             with nc.allow_non_contiguous_dma(reason="one threshold to a partition"):
                 nc.sync.dma_start(out=tau_raw[:, :, 0], in_=tau.rearrange("(j p) -> p j", p=P))
 
+        def split_words(i):
+            w_split[i] = sb.tile([P, G, 2, P], F32, name="w_split%d" % i, tag="w_split%d" % (i % 3), align_bytes=64)
+            words = w_rows[i][:].bitcast(F32).rearrange("p (g m u) -> p g u m", g=G, u=2)
+            for half in range(2):
+                gs = slice(2 * half, 2 * half + 2)
+                nc.vector.tensor_copy(out=w_split[i][:, gs, :, :], in_=words[:, gs, :, :])
+
         def transpose_w(i, half):
             bank = next_bank()
             t_banks[i, half] = bank
-            words = w_rows[i][:].bitcast(F32)
             for gl in range(2):
-                g = 2 * half + gl
                 for u in range(2):
                     slot = 2 * gl + u
-                    nc.tensor.transpose(bank[:, slot * P:(slot + 1) * P],
-                                        words[:, 256 * g + u:256 * (g + 1):2], ident[:])
+                    nc.tensor.transpose(bank[:, slot * P:(slot + 1) * P], w_split[i][:, 2 * half + gl, u, :], ident[:])
 
         def copy_w(i, half):
             dst = w_t[i][:, 2 * half:2 * half + 2, :, :].bitcast(F32)
             nc.scalar.copy(out=dst, in_=t_banks[i, half][:].rearrange("p (g u m) -> p g m u", g=2, u=2))
 
-        def quant_w(i, g0, g1):
-            nc.vector.quantize_mx(out=w_codes[i][:, g0 * P:g1 * P].bitcast(E4),
-                                  scales=w_scale[i][:, g0 * P:g1 * P],
-                                  in_=w_t[i][:, g0:g1, :, :].rearrange("p g m t -> p (g m t)"))
+        def quant_w(i):
+            for g0, g1 in ((0, 2), (2, 4)):
+                nc.vector.quantize_mx(out=w_codes[i][:, g0 * P:g1 * P].bitcast(E4),
+                                      scales=w_scale[i][:, g0 * P:g1 * P],
+                                      in_=w_t[i][:, g0:g1, :, :].rearrange("p g m t -> p (g m t)"))
 
-        def stage1(i, c):
-            bank = next_bank()
-            r_bank[i, c] = bank
-            for g in range(G):
-                nc.tensor.matmul_mx(out=bank[:],
-                                    lhsT=w_codes[i][:, g * P:(g + 1) * P].bitcast(E4),
-                                    lhsT_scale=w_scale[i][:, g * P:(g + 1) * P],
-                                    rhs=y_codes[c][:, g, :].bitcast(E5),
-                                    rhs_scale=y_scale[c][:, g, :],
-                                    start=(g == 0), stop=(g == G - 1))
+        def stage1(i, c, halves=(0, 1)):
+            if 0 in halves:
+                r_bank[i, c] = next_bank()
+            for half in halves:
+                for g in (2 * half, 2 * half + 1):
+                    nc.tensor.matmul_mx(out=r_bank[i, c][:],
+                                        lhsT=w_codes[i][:, g * P:(g + 1) * P].bitcast(E4),
+                                        lhsT_scale=w_scale[i][:, g * P:(g + 1) * P],
+                                        rhs=y_codes[c][:, g, :].bitcast(E5),
+                                        rhs_scale=y_scale[c][:, g, :],
+                                        start=(g == 0), stop=(g == G - 1))
 
-        def weigh(i, c):
+        def weigh(i, c, n0=0, n1=N):
             h, t = divmod(i, PACK)
-            nc.vector.tensor_tensor(out=z_rows[h, c][:, t, :], in0=r_bank[i, c][:], in1=s_sb[h, c][:, t, :],
-                                    op=ALU.mult)
+            nc.vector.tensor_tensor(out=z_rows[h, c][:, t, n0:n1], in0=r_bank[i, c][:, n0:n1],
+                                    in1=s_sb[h, c][:, t, n0:n1], op=ALU.mult)
 
-        def interleave(copy, dst, src):
-            copy(out=dst[:].rearrange("p (n i) t -> p n t i", i=4),
-                 in_=src[:].rearrange("p t (n i) -> p n t i", i=4))
+        def interleave(copy, dst, src, n0=0, n1=N):
+            copy(out=dst[:, n0:n1, :].rearrange("p (n i) t -> p n t i", i=4),
+                 in_=src[:, :, n0:n1].rearrange("p t (n i) -> p n t i", i=4))
 
-        def quant_z(h, c):
-            nc.vector.quantize_mx(out=z_codes[h, c][:].bitcast(E5), scales=z_scale[h, c][:],
-                                  in_=z_il[h, c][:].rearrange("p n t -> p (n t)"))
+        def quant_z(h, c, n0=0, n1=N):
+            nc.vector.quantize_mx(out=z_codes[h, c][:, n0:n1].bitcast(E5), scales=z_scale[h, c][:, n0:n1],
+                                  in_=z_il[h, c][:, n0:n1, :].rearrange("p n t -> p (n t)"))
+
+        def idle_operands():
+            nc.vector.memset(idle[:].bitcast(I32), 0)
+            zeros = idle[:, 800:864].bitcast(BF16)
+            nc.vector.quantize_mx(out=idle[:, 0:32].bitcast(E5), scales=idle[:, 640:648].bitcast(U8), in_=zeros)
+            nc.vector.quantize_mx(out=idle[:, 512:544].bitcast(E4), scales=idle[:, 768:776].bitcast(U8), in_=zeros)
+
+        def keep_clock(passes):
+            bank = next_bank()
+            for n in range(passes):
+                nc.tensor.matmul_mx(out=bank[:], lhsT=idle[:, 512:640].bitcast(E4),
+                                    lhsT_scale=idle[:, 768:800].bitcast(U8),
+                                    rhs=idle[:, 0:512].bitcast(E5), rhs_scale=idle[:, 640:768].bitcast(U8),
+                                    start=True, stop=True)
 
         def quant_d(h):
             nc.vector.quantize_mx(out=d_codes[h][:].bitcast(E4), scales=d_scale[h][:],
@@ -177,99 +200,113 @@ def tile_parity_fault_isolation_e3_kernel(tc, y_words, y_scales, w, sens, d, tau
         make_identity(nc, ident[:])
         nc.vector.memset(warm[:], 0.0)
         nc.scalar.activation(out=warm_out[:], in_=warm[:], func=ACT.Abs)
+        idle_operands()
         for c in range(2):
             nc.vector.memset(y_scale[c][:].rearrange("p g n -> p (g n)").bitcast(I32), 0)
 
-        load_w(0, 0, K // 2)
-        load_w(0, K // 2, K)
-        load_w(1, 0, K)
+        for i in range(4):
+            load_w(i)
         load_y_scale(0)
-        load_y(0, 0, 2)
-        load_y(0, 2, 4)
-        load_w(2, 0, K)
-        load_w(3, 0, K)
+        load_y(0, 0)
+        load_w(4)
+        load_y(0, 1)
         load_sens(0, 0)
-        load_w(4, 0, K)
-        load_w(5, 0, K)
+        load_w(5)
+        load_w(6)
+        load_w(7)
         load_d(0)
-        load_w(6, 0, K)
-        load_w(7, 0, K)
         load_sens(1, 0)
-        load_d(1)
         load_y_scale(1)
-        load_y(1, 0, 2)
-        load_y(1, 2, 4)
+        load_y(1, 0)
+        load_d(1)
+        load_y(1, 1)
         load_sens(0, 1)
         load_tau()
         load_sens(1, 1)
 
+        keep_clock(4)
+        split_words(0)
         turn(0)
-        quant_w(0, 0, 2)
-        quant_w(0, 2, 4)
-        turn(1)
-        quant_w(1, 0, G)
-        stage1(0, 0)
-        turn(2)
-        turn(3)
-        quant_w(2, 0, G)
-        stage1(1, 0)
+        for i in (1, 2, 3):
+            keep_clock(1)
+            split_words(i)
+            quant_w(i - 1)
+            turn(i)
+        quant_w(3)
+        split_words(4)
+        for i in range(4):
+            stage1(i, 0, (0,))
+        turn(4)
+        quant_w(4)
+        for i in range(4):
+            stage1(i, 0, (1,))
         weigh(0, 0)
-        quant_w(3, 0, G)
-        stage1(2, 0)
+        split_words(5)
+        turn(5)
         weigh(1, 0)
         weigh(2, 0)
-        turn(4)
-        turn(5)
-        quant_w(4, 0, G)
-        quant_w(5, 0, G)
-        interleave(s_copy, d_il[0], d_rows[0])
-        stage1(3, 0)
-        weigh(3, 0)
         stage1(4, 0)
-        weigh(4, 0)
-        interleave(v_copy, z_il[0, 0], z_rows[0, 0])
+        split_words(6)
+        weigh(3, 0)
         turn(6)
+        split_words(7)
         turn(7)
-        quant_d(0)
-        quant_w(6, 0, G)
+        quant_w(5)
+        quant_w(6)
+        stage1(5, 0)
+        weigh(4, 0)
+        quant_w(7)
+        weigh(5, 0)
+        interleave(s_copy, d_il[0], d_rows[0])
+        interleave(v_copy, z_il[0, 0], z_rows[0, 0])
+        stage1(6, 0)
+        stage1(7, 0)
+        weigh(6, 0)
+        weigh(7, 0)
         quant_z(0, 0)
-        quant_w(7, 0, G)
+        quant_d(0)
         interleave(s_copy, d_il[1], d_rows[1])
-        for i in (5, 6, 7):
-            stage1(i, 0)
-            weigh(i, 0)
         interleave(s_copy, z_il[1, 0], z_rows[1, 0])
+        for half in range(2):
+            for i in range(4):
+                stage1(i, 1, (half,))
+        weigh(0, 1)
         quant_d(1)
-        nc.vector.tensor_copy(out=tau_sb[:], in_=tau_raw[:, :, 0])
-        for i in (0, 1, 2):
-            stage1(i, 1)
-            weigh(i, 1)
-        quant_z(1, 0)
-        stage1(3, 1)
+        weigh(1, 1)
+        weigh(2, 1)
         weigh(3, 1)
-        stage2(0, 0, 0)
-        stage2(0, 0, 1)
-        magnitude(0, 0)
-        interleave(s_copy, z_il[0, 1], z_rows[0, 1])
+        nc.vector.tensor_copy(out=tau_sb[:], in_=tau_raw[:, :, 0])
+        quant_z(1, 0)
+        interleave(s_copy, z_il[0, 1], z_rows[0, 1], 0, N // 2)
+        interleave(v_copy, z_il[0, 1], z_rows[0, 1], N // 2, N)
         stage1(4, 1)
-        threshold(0, 0)
         weigh(4, 1)
         stage1(5, 1)
         weigh(5, 1)
+        stage2(0, 0, 0)
+        stage2(0, 0, 1)
+        magnitude(0, 0)
+        quant_z(0, 1)
         stage1(6, 1)
         weigh(6, 1)
-        quant_z(0, 1)
+        stage2(0, 1, 0)
+        stage2(0, 1, 1)
+        magnitude(0, 1)
+        threshold(0, 0)
+        threshold(0, 1)
         stage1(7, 1)
-        weigh(7, 1)
-        interleave(v_copy, z_il[1, 1], z_rows[1, 1])
-        for j in (1, 2, 3):
+        weigh(7, 1, 0, N // 2)
+        weigh(7, 1, N // 2, N)
+        interleave(s_copy, z_il[1, 1], z_rows[1, 1], 0, N // 4)
+        interleave(v_copy, z_il[1, 1], z_rows[1, 1], N // 4, N // 2)
+        interleave(v_copy, z_il[1, 1], z_rows[1, 1], N // 2, N)
+        quant_z(1, 1, 0, N // 2)
+        quant_z(1, 1, N // 2, N)
+        for j in (2, 3):
             stage2(0, j, 0)
             stage2(0, j, 1)
             magnitude(0, j)
-        threshold(0, 1)
-        quant_z(1, 1)
-        threshold(0, 2)
-        threshold(0, 3)
+            threshold(0, j)
         for j in range(4):
             stage2(1, j, 0)
         for j in range(4):

@@ -33,13 +33,17 @@ def tile_parity_fault_isolation_e3_kernel(tc, y_words, y_scales, w, sens, d, tau
         def sbuf(name, shape, dtype):
             return sb.tile(shape, dtype, name=name, align_bytes=64)
 
-        banks_taken = []
+        free_banks = list(range(BANKS))
+        bank_of = {}
 
-        def next_bank():
-            n = len(banks_taken)
-            bank = ps.tile([P, N], F32, name="bank%d" % n, tag="bank%d" % (n % BANKS))
-            banks_taken.append(bank)
+        def take_bank(key):
+            n = free_banks.pop(0)
+            bank = ps.tile([P, N], F32, name="bank_" + "_".join(str(x) for x in key), tag="bank%d" % n)
+            bank_of[key] = (n, bank)
             return bank
+
+        def release_bank(key):
+            free_banks.append(bank_of[key][0])
 
         ident = sbuf("ident", [P, P], F32)
         warm = sbuf("warm", [P, 1], F32)
@@ -63,11 +67,8 @@ def tile_parity_fault_isolation_e3_kernel(tc, y_words, y_scales, w, sens, d, tau
         d_codes = [sbuf("d_codes%d" % h, [P, F], U32) for h in range(2)]
         d_scale = [sbuf("d_scale%d" % h, [P, F], U8) for h in range(2)]
         tau_raw = sbuf("tau_raw", [P, 4, 2], BF16)
-        tau_sb = sbuf("tau_sb", [P, 4], F32)
+        neg_tau = sbuf("neg_tau", [P, 4], F32)
 
-        t_banks = {}
-        r_bank = {}
-        o_bank = {}
         mag = {}
         res = {}
 
@@ -84,8 +85,7 @@ def tile_parity_fault_isolation_e3_kernel(tc, y_words, y_scales, w, sens, d, tau
                 src = y_scales[:, 4 * q:4 * q + 4, cols(c)].rearrange("g r n -> r g n")
                 nc.sync.dma_start(out=y_scale[c][32 * q:32 * q + 4, :, :].bitcast(I32), in_=src.bitcast(I32))
 
-        def load_y(c, half):
-            g0, g1 = 2 * half, 2 * half + 2
+        def load_y(c, g0, g1):
             src = y_words.rearrange("g p n t -> p g (n t)")[:, g0:g1, c * N * PACK:(c + 1) * N * PACK]
             nc.sync.dma_start(out=y_codes[c][:, g0:g1, :].bitcast(I32), in_=src.bitcast(I32))
 
@@ -101,47 +101,51 @@ def tile_parity_fault_isolation_e3_kernel(tc, y_words, y_scales, w, sens, d, tau
             with nc.allow_non_contiguous_dma(reason="one threshold to a partition"):
                 nc.sync.dma_start(out=tau_raw[:, :, 0], in_=tau.rearrange("(j p) -> p j", p=P))
 
-        def split_words(i):
+        def split_words(i, copies):
             w_split[i] = sb.tile([P, G, 2, P], F32, name="w_split%d" % i, tag="w_split%d" % (i % 3), align_bytes=64)
             words = w_rows[i][:].bitcast(F32).rearrange("p (g m u) -> p g u m", g=G, u=2)
-            for half in range(2):
+            for half, copy in enumerate(copies):
                 gs = slice(2 * half, 2 * half + 2)
-                nc.vector.tensor_copy(out=w_split[i][:, gs, :, :], in_=words[:, gs, :, :])
+                copy(out=w_split[i][:, gs, :, :], in_=words[:, gs, :, :])
 
-        def transpose_w(i, half):
-            bank = next_bank()
-            t_banks[i, half] = bank
-            for gl in range(2):
-                for u in range(2):
-                    slot = 2 * gl + u
-                    nc.tensor.transpose(bank[:, slot * P:(slot + 1) * P], w_split[i][:, 2 * half + gl, u, :], ident[:])
+        def transpose_w(i):
+            for half in range(2):
+                bank = take_bank(("t", i, half))
+                for gl in range(2):
+                    for u in range(2):
+                        slot = 2 * gl + u
+                        nc.tensor.transpose(bank[:, slot * P:(slot + 1) * P], w_split[i][:, 2 * half + gl, u, :],
+                                            ident[:])
 
         def copy_w(i, half):
             dst = w_t[i][:, 2 * half:2 * half + 2, :, :].bitcast(F32)
-            nc.scalar.copy(out=dst, in_=t_banks[i, half][:].rearrange("p (g u m) -> p g m u", g=2, u=2))
+            bank = bank_of["t", i, half][1]
+            nc.scalar.copy(out=dst, in_=bank[:].rearrange("p (g u m) -> p g m u", g=2, u=2))
+            release_bank(("t", i, half))
 
-        def quant_w(i):
-            for g0, g1 in ((0, 2), (2, 4)):
-                nc.vector.quantize_mx(out=w_codes[i][:, g0 * P:g1 * P].bitcast(E4),
-                                      scales=w_scale[i][:, g0 * P:g1 * P],
-                                      in_=w_t[i][:, g0:g1, :, :].rearrange("p g m t -> p (g m t)"))
+        def quant_w(i, half):
+            g0, g1 = 2 * half, 2 * half + 2
+            nc.vector.quantize_mx(out=w_codes[i][:, g0 * P:g1 * P].bitcast(E4),
+                                  scales=w_scale[i][:, g0 * P:g1 * P],
+                                  in_=w_t[i][:, g0:g1, :, :].rearrange("p g m t -> p (g m t)"))
 
-        def stage1(i, c, halves=(0, 1)):
-            if 0 in halves:
-                r_bank[i, c] = next_bank()
-            for half in halves:
-                for g in (2 * half, 2 * half + 1):
-                    nc.tensor.matmul_mx(out=r_bank[i, c][:],
-                                        lhsT=w_codes[i][:, g * P:(g + 1) * P].bitcast(E4),
-                                        lhsT_scale=w_scale[i][:, g * P:(g + 1) * P],
-                                        rhs=y_codes[c][:, g, :].bitcast(E5),
-                                        rhs_scale=y_scale[c][:, g, :],
-                                        start=(g == 0), stop=(g == G - 1))
+        def stage1(i, c, groups=range(G)):
+            for g in groups:
+                if g == 0:
+                    take_bank(("r", i, c))
+                nc.tensor.matmul_mx(out=bank_of["r", i, c][1][:],
+                                    lhsT=w_codes[i][:, g * P:(g + 1) * P].bitcast(E4),
+                                    lhsT_scale=w_scale[i][:, g * P:(g + 1) * P],
+                                    rhs=y_codes[c][:, g, :].bitcast(E5),
+                                    rhs_scale=y_scale[c][:, g, :],
+                                    start=(g == 0), stop=(g == G - 1))
 
         def weigh(i, c, n0=0, n1=N):
             h, t = divmod(i, PACK)
-            nc.vector.tensor_tensor(out=z_rows[h, c][:, t, n0:n1], in0=r_bank[i, c][:, n0:n1],
+            nc.vector.tensor_tensor(out=z_rows[h, c][:, t, n0:n1], in0=bank_of["r", i, c][1][:, n0:n1],
                                     in1=s_sb[h, c][:, t, n0:n1], op=ALU.mult)
+            if n1 == N:
+                release_bank(("r", i, c))
 
         def interleave(copy, dst, src, n0=0, n1=N):
             copy(out=dst[:, n0:n1, :].rearrange("p (n i) t -> p n t i", i=4),
@@ -158,7 +162,8 @@ def tile_parity_fault_isolation_e3_kernel(tc, y_words, y_scales, w, sens, d, tau
             nc.vector.quantize_mx(out=idle[:, 512:544].bitcast(E4), scales=idle[:, 768:776].bitcast(U8), in_=zeros)
 
         def keep_clock(passes):
-            bank = next_bank()
+            bank = take_bank(("idle", len(bank_of)))
+            release_bank(("idle", len(bank_of) - 1))
             for n in range(passes):
                 nc.tensor.matmul_mx(out=bank[:], lhsT=idle[:, 512:640].bitcast(E4),
                                     lhsT_scale=idle[:, 768:800].bitcast(U8),
@@ -171,8 +176,8 @@ def tile_parity_fault_isolation_e3_kernel(tc, y_words, y_scales, w, sens, d, tau
 
         def stage2(c, j, h):
             if h == 0:
-                o_bank[c, j] = next_bank()
-            nc.tensor.matmul_mx(out=o_bank[c, j][:],
+                take_bank(("o", c, j))
+            nc.tensor.matmul_mx(out=bank_of["o", c, j][1][:],
                                 lhsT=d_codes[h][:, j * P:(j + 1) * P].bitcast(E4),
                                 lhsT_scale=d_scale[h][:, j * P:(j + 1) * P],
                                 rhs=z_codes[h, c][:].bitcast(E5),
@@ -181,18 +186,22 @@ def tile_parity_fault_isolation_e3_kernel(tc, y_words, y_scales, w, sens, d, tau
 
         def magnitude(c, j):
             mag[c, j] = sbuf("mag%d%d" % (c, j), [P, N], F32)
-            nc.scalar.activation(out=mag[c, j][:], in_=o_bank[c, j][:], func=ACT.Abs)
+            nc.scalar.activation(out=mag[c, j][:], in_=bank_of["o", c, j][1][:], func=ACT.Abs)
+            release_bank(("o", c, j))
 
-        def threshold(c, j):
+        def threshold(c, j, on_scalar=False):
             res[c, j] = sbuf("res%d%d" % (c, j), [P, N], F32)
-            nc.vector.tensor_scalar(out=res[c, j][:], in0=mag[c, j][:], scalar1=tau_sb[:, j:j + 1], scalar2=0.0,
-                                    op0=ALU.subtract, op1=ALU.max)
+            if on_scalar:
+                nc.scalar.activation(out=res[c, j][:], in_=mag[c, j][:], func=ACT.Relu, bias=neg_tau[:, j:j + 1])
+            else:
+                nc.vector.tensor_scalar(out=res[c, j][:], in0=mag[c, j][:], scalar1=neg_tau[:, j:j + 1],
+                                        scalar2=0.0, op0=ALU.add, op1=ALU.max)
             nc.sync.dma_start(out=out[j * P:(j + 1) * P, cols(c)], in_=res[c, j][:])
 
         def turn(i):
-            for half in range(2):
-                transpose_w(i, half)
-                copy_w(i, half)
+            transpose_w(i)
+            copy_w(i, 0)
+            copy_w(i, 1)
 
         v_copy = nc.vector.tensor_copy
         s_copy = nc.scalar.copy
@@ -207,93 +216,106 @@ def tile_parity_fault_isolation_e3_kernel(tc, y_words, y_scales, w, sens, d, tau
         for i in range(4):
             load_w(i)
         load_y_scale(0)
-        load_y(0, 0)
+        load_y(0, 0, 1)
+        load_y(0, 1, 2)
         load_w(4)
-        load_y(0, 1)
-        load_sens(0, 0)
+        load_y(0, 2, 4)
         load_w(5)
+        load_sens(0, 0)
         load_w(6)
         load_w(7)
-        load_d(0)
         load_sens(1, 0)
         load_y_scale(1)
-        load_y(1, 0)
+        load_y(1, 0, 2)
+        load_d(0)
         load_d(1)
-        load_y(1, 1)
+        load_y(1, 2, 4)
         load_sens(0, 1)
-        load_tau()
         load_sens(1, 1)
+        load_tau()
 
+        on_vector = (v_copy, v_copy)
+        shared = (v_copy, s_copy)
         keep_clock(4)
-        split_words(0)
+        split_words(0, on_vector)
         turn(0)
         for i in (1, 2, 3):
             keep_clock(1)
-            split_words(i)
-            quant_w(i - 1)
+            split_words(i, on_vector)
+            quant_w(i - 1, 0)
             turn(i)
-        quant_w(3)
-        split_words(4)
-        for i in range(4):
-            stage1(i, 0, (0,))
+        quant_w(0, 1)
+        for g in (0, 1):
+            for i in (0, 1, 2):
+                stage1(i, 0, (g,))
+        quant_w(3, 0)
+        stage1(3, 0, (0, 1))
+        quant_w(1, 1)
+        split_words(4, on_vector)
         turn(4)
-        quant_w(4)
+        quant_w(2, 1)
+        quant_w(3, 1)
         for i in range(4):
-            stage1(i, 0, (1,))
+            stage1(i, 0, (2, 3))
+        split_words(5, shared)
+        quant_w(4, 0)
+        quant_w(4, 1)
+        transpose_w(5)
         weigh(0, 0)
-        split_words(5)
-        turn(5)
+        copy_w(5, 0)
         weigh(1, 0)
-        weigh(2, 0)
+        copy_w(5, 1)
         stage1(4, 0)
-        split_words(6)
-        weigh(3, 0)
-        turn(6)
-        split_words(7)
-        turn(7)
-        quant_w(5)
-        quant_w(6)
+        split_words(6, shared)
+        weigh(2, 0)
+        transpose_w(6)
+        quant_w(5, 0)
+        quant_w(5, 1)
+        copy_w(6, 0)
         stage1(5, 0)
+        split_words(7, shared)
+        quant_w(6, 0)
+        copy_w(6, 1)
+        weigh(3, 0)
         weigh(4, 0)
-        quant_w(7)
-        weigh(5, 0)
-        interleave(s_copy, d_il[0], d_rows[0])
-        interleave(v_copy, z_il[0, 0], z_rows[0, 0])
+        turn(7)
+        quant_w(6, 1)
         stage1(6, 0)
+        quant_w(7, 0)
+        quant_w(7, 1)
         stage1(7, 0)
+        interleave(v_copy, z_il[0, 0], z_rows[0, 0], 0, N // 2)
+        interleave(s_copy, z_il[0, 0], z_rows[0, 0], N // 2, N)
+        weigh(5, 0)
+        interleave(s_copy, d_il[0], d_rows[0], 0, F // 2)
+        interleave(v_copy, d_il[0], d_rows[0], F // 2, F)
+        for i in range(4):
+            stage1(i, 1, (0, 1))
         weigh(6, 0)
         weigh(7, 0)
         quant_z(0, 0)
         quant_d(0)
         interleave(s_copy, d_il[1], d_rows[1])
         interleave(s_copy, z_il[1, 0], z_rows[1, 0])
-        for half in range(2):
-            for i in range(4):
-                stage1(i, 1, (half,))
-        weigh(0, 1)
+        for i in range(4):
+            stage1(i, 1, (2, 3))
+            weigh(i, 1)
+        interleave(s_copy, z_il[0, 1], z_rows[0, 1])
         quant_d(1)
-        weigh(1, 1)
-        weigh(2, 1)
-        weigh(3, 1)
-        nc.vector.tensor_copy(out=tau_sb[:], in_=tau_raw[:, :, 0])
         quant_z(1, 0)
-        interleave(s_copy, z_il[0, 1], z_rows[0, 1], 0, N // 2)
-        interleave(v_copy, z_il[0, 1], z_rows[0, 1], N // 2, N)
-        stage1(4, 1)
-        weigh(4, 1)
-        stage1(5, 1)
-        weigh(5, 1)
-        stage2(0, 0, 0)
-        stage2(0, 0, 1)
-        magnitude(0, 0)
-        quant_z(0, 1)
+        nc.vector.tensor_scalar(out=neg_tau[:], in0=tau_raw[:, :, 0], scalar1=-1.0, scalar2=None, op0=ALU.mult)
+        for i in (4, 5):
+            stage1(i, 1)
+            weigh(i, 1)
         stage1(6, 1)
+        quant_z(0, 1)
         weigh(6, 1)
-        stage2(0, 1, 0)
-        stage2(0, 1, 1)
-        magnitude(0, 1)
-        threshold(0, 0)
-        threshold(0, 1)
+        for j in (0, 1):
+            stage2(0, j, 0)
+            stage2(0, j, 1)
+            magnitude(0, j)
+        for j in (0, 1):
+            threshold(0, j, on_scalar=True)
         stage1(7, 1)
         weigh(7, 1, 0, N // 2)
         weigh(7, 1, N // 2, N)

from contextlib import ExitStack

import concourse.mybir as mybir
from concourse.masks import make_identity

K, B, PR, F = 2048, 1024, 1024, 512
FLOPS = 2 * PR * K * B + 2 * F * PR * B

F32 = mybir.dt.float32
BF16 = mybir.dt.bfloat16
I32 = mybir.dt.int32
U32 = mybir.dt.uint32
U8 = mybir.dt.uint8
E4 = mybir.dt.float8_e4m3fn_x4
E5 = mybir.dt.float8_e5m2_x4
ALU = mybir.AluOpType
ACT = mybir.ActivationFunctionType

P = 128
PACK = 4
N = 512
G = K // 512
BANKS = 8


def tile_parity_fault_isolation_e3_kernel(tc, y_words, y_scales, w, sens, d, tau, out):
    nc = tc.nc
    with ExitStack() as ctx:
        sb = ctx.enter_context(tc.tile_pool(name="sb", bufs=1))
        ps = ctx.enter_context(tc.psum_pool(name="ps", bufs=1))
        ctx.enter_context(tc.manual_schedule())

        def sbuf(name, shape, dtype):
            return sb.tile(shape, dtype, name=name, align_bytes=64)

        free_banks = list(range(BANKS))
        bank_of = {}

        def take_bank(key):
            n = free_banks.pop(0)
            bank = ps.tile([P, N], F32, name="bank_" + "_".join(str(x) for x in key), tag="bank%d" % n)
            bank_of[key] = (n, bank)
            return bank

        def release_bank(key):
            free_banks.append(bank_of[key][0])

        ident = sbuf("ident", [P, P], F32)
        warm = sbuf("warm", [P, 1], F32)
        warm_out = sbuf("warm_out", [P, 1], F32)
        w_rows = [sbuf("w_rows%d" % i, [P, K], BF16) for i in range(8)]
        w_split = {}
        idle = sbuf("idle", [P, 864], U32)
        w_t = [sbuf("w_t%d" % i, [P, G, P, PACK], BF16) for i in range(8)]
        w_codes = [sbuf("w_codes%d" % i, [P, G * P], U32) for i in range(8)]
        w_scale = [sbuf("w_scale%d" % i, [P, G * P], U8) for i in range(8)]
        y_codes = [sbuf("y_codes%d" % c, [P, G, N], U32) for c in range(2)]
        y_scale = [sbuf("y_scale%d" % c, [P, G, N], U8) for c in range(2)]
        hc = [(h, c) for h in range(2) for c in range(2)]
        s_sb = {(h, c): sbuf("s%d%d" % (h, c), [P, PACK, N], BF16) for h, c in hc}
        z_rows = {(h, c): sbuf("z_rows%d%d" % (h, c), [P, PACK, N], BF16) for h, c in hc}
        z_il = {(h, c): sbuf("z_il%d%d" % (h, c), [P, N, PACK], BF16) for h, c in hc}
        z_codes = {(h, c): sbuf("z_codes%d%d" % (h, c), [P, N], U32) for h, c in hc}
        z_scale = {(h, c): sbuf("z_scale%d%d" % (h, c), [P, N], U8) for h, c in hc}
        d_rows = [sbuf("d_rows%d" % h, [P, PACK, F], BF16) for h in range(2)]
        d_il = [sbuf("d_il%d" % h, [P, F, PACK], BF16) for h in range(2)]
        d_codes = [sbuf("d_codes%d" % h, [P, F], U32) for h in range(2)]
        d_scale = [sbuf("d_scale%d" % h, [P, F], U8) for h in range(2)]
        tau_raw = sbuf("tau_raw", [P, 4, 2], BF16)
        neg_tau = sbuf("neg_tau", [P, 4], F32)

        mag = {}
        res = {}

        def cols(c):
            return slice(c * N, (c + 1) * N)

        def load_w(i):
            h, t = divmod(i, PACK)
            rows = w[h * 512:(h + 1) * 512, :].rearrange("(m t) k -> t m k", t=PACK)[t]
            nc.sync.dma_start(out=w_rows[i][:], in_=rows)

        def load_y_scale(c):
            for q in range(4):
                src = y_scales[:, 4 * q:4 * q + 4, cols(c)].rearrange("g r n -> r g n")
                nc.sync.dma_start(out=y_scale[c][32 * q:32 * q + 4, :, :].bitcast(I32), in_=src.bitcast(I32))

        def load_y(c, g0, g1):
            src = y_words.rearrange("g p n t -> p g (n t)")[:, g0:g1, c * N * PACK:(c + 1) * N * PACK]
            nc.sync.dma_start(out=y_codes[c][:, g0:g1, :].bitcast(I32), in_=src.bitcast(I32))

        def load_sens(h, c):
            src = sens[h * 512:(h + 1) * 512, cols(c)].rearrange("(p t) n -> p t n", t=PACK)
            nc.sync.dma_start(out=s_sb[h, c][:], in_=src)

        def load_d(h):
            src = d[h * 512:(h + 1) * 512, :].rearrange("(p t) f -> p t f", t=PACK)
            nc.sync.dma_start(out=d_rows[h][:], in_=src)

        def load_tau():
            with nc.allow_non_contiguous_dma(reason="one threshold to a partition"):
                nc.sync.dma_start(out=tau_raw[:, :, 0], in_=tau.rearrange("(j p) -> p j", p=P))

        def split_words(i, copies):
            w_split[i] = sb.tile([P, G, 2, P], F32, name="w_split%d" % i, tag="w_split%d" % (i % 3), align_bytes=64)
            words = w_rows[i][:].bitcast(F32).rearrange("p (g m u) -> p g u m", g=G, u=2)
            for half, copy in enumerate(copies):
                gs = slice(2 * half, 2 * half + 2)
                copy(out=w_split[i][:, gs, :, :], in_=words[:, gs, :, :])

        def transpose_w(i):
            for half in range(2):
                bank = take_bank(("t", i, half))
                for gl in range(2):
                    for u in range(2):
                        slot = 2 * gl + u
                        nc.tensor.transpose(bank[:, slot * P:(slot + 1) * P], w_split[i][:, 2 * half + gl, u, :],
                                            ident[:])

        def copy_w(i, half):
            dst = w_t[i][:, 2 * half:2 * half + 2, :, :].bitcast(F32)
            bank = bank_of["t", i, half][1]
            nc.scalar.copy(out=dst, in_=bank[:].rearrange("p (g u m) -> p g m u", g=2, u=2))
            release_bank(("t", i, half))

        def quant_w(i, half):
            g0, g1 = 2 * half, 2 * half + 2
            nc.vector.quantize_mx(out=w_codes[i][:, g0 * P:g1 * P].bitcast(E4),
                                  scales=w_scale[i][:, g0 * P:g1 * P],
                                  in_=w_t[i][:, g0:g1, :, :].rearrange("p g m t -> p (g m t)"))

        def stage1(i, c, groups=range(G)):
            for g in groups:
                if g == 0:
                    take_bank(("r", i, c))
                nc.tensor.matmul_mx(out=bank_of["r", i, c][1][:],
                                    lhsT=w_codes[i][:, g * P:(g + 1) * P].bitcast(E4),
                                    lhsT_scale=w_scale[i][:, g * P:(g + 1) * P],
                                    rhs=y_codes[c][:, g, :].bitcast(E5),
                                    rhs_scale=y_scale[c][:, g, :],
                                    start=(g == 0), stop=(g == G - 1))

        def weigh(i, c, n0=0, n1=N):
            h, t = divmod(i, PACK)
            nc.vector.tensor_tensor(out=z_rows[h, c][:, t, n0:n1], in0=bank_of["r", i, c][1][:, n0:n1],
                                    in1=s_sb[h, c][:, t, n0:n1], op=ALU.mult)
            if n1 == N:
                release_bank(("r", i, c))

        def interleave(copy, dst, src, n0=0, n1=N):
            copy(out=dst[:, n0:n1, :].rearrange("p (n i) t -> p n t i", i=4),
                 in_=src[:, :, n0:n1].rearrange("p t (n i) -> p n t i", i=4))

        def quant_z(h, c, n0=0, n1=N):
            nc.vector.quantize_mx(out=z_codes[h, c][:, n0:n1].bitcast(E5), scales=z_scale[h, c][:, n0:n1],
                                  in_=z_il[h, c][:, n0:n1, :].rearrange("p n t -> p (n t)"))

        def idle_operands():
            nc.vector.memset(idle[:].bitcast(I32), 0)
            zeros = idle[:, 800:864].bitcast(BF16)
            nc.vector.quantize_mx(out=idle[:, 0:32].bitcast(E5), scales=idle[:, 640:648].bitcast(U8), in_=zeros)
            nc.vector.quantize_mx(out=idle[:, 512:544].bitcast(E4), scales=idle[:, 768:776].bitcast(U8), in_=zeros)

        def keep_clock(passes):
            bank = take_bank(("idle", len(bank_of)))
            release_bank(("idle", len(bank_of) - 1))
            for n in range(passes):
                nc.tensor.matmul_mx(out=bank[:], lhsT=idle[:, 512:640].bitcast(E4),
                                    lhsT_scale=idle[:, 768:800].bitcast(U8),
                                    rhs=idle[:, 0:512].bitcast(E5), rhs_scale=idle[:, 640:768].bitcast(U8),
                                    start=True, stop=True)

        def quant_d(h):
            nc.vector.quantize_mx(out=d_codes[h][:].bitcast(E4), scales=d_scale[h][:],
                                  in_=d_il[h][:].rearrange("p f t -> p (f t)"))

        def stage2(c, j, h):
            if h == 0:
                take_bank(("o", c, j))
            nc.tensor.matmul_mx(out=bank_of["o", c, j][1][:],
                                lhsT=d_codes[h][:, j * P:(j + 1) * P].bitcast(E4),
                                lhsT_scale=d_scale[h][:, j * P:(j + 1) * P],
                                rhs=z_codes[h, c][:].bitcast(E5),
                                rhs_scale=z_scale[h, c][:],
                                start=(h == 0), stop=(h == 1))

        def magnitude(c, j):
            mag[c, j] = sbuf("mag%d%d" % (c, j), [P, N], F32)
            nc.scalar.activation(out=mag[c, j][:], in_=bank_of["o", c, j][1][:], func=ACT.Abs)
            release_bank(("o", c, j))

        def threshold(c, j, on_scalar=False):
            res[c, j] = sbuf("res%d%d" % (c, j), [P, N], F32)
            if on_scalar:
                nc.scalar.activation(out=res[c, j][:], in_=mag[c, j][:], func=ACT.Relu, bias=neg_tau[:, j:j + 1])
            else:
                nc.vector.tensor_scalar(out=res[c, j][:], in0=mag[c, j][:], scalar1=neg_tau[:, j:j + 1],
                                        scalar2=0.0, op0=ALU.add, op1=ALU.max)
            nc.sync.dma_start(out=out[j * P:(j + 1) * P, cols(c)], in_=res[c, j][:])

        def turn(i):
            transpose_w(i)
            copy_w(i, 0)
            copy_w(i, 1)

        v_copy = nc.vector.tensor_copy
        s_copy = nc.scalar.copy

        make_identity(nc, ident[:])
        nc.vector.memset(warm[:], 0.0)
        nc.scalar.activation(out=warm_out[:], in_=warm[:], func=ACT.Abs)
        idle_operands()
        for c in range(2):
            nc.vector.memset(y_scale[c][:].rearrange("p g n -> p (g n)").bitcast(I32), 0)

        for i in range(4):
            load_w(i)
        load_y_scale(0)
        load_y(0, 0, 1)
        load_y(0, 1, 2)
        load_w(4)
        load_y(0, 2, 4)
        load_w(5)
        load_sens(0, 0)
        load_w(6)
        load_w(7)
        load_sens(1, 0)
        load_y_scale(1)
        load_y(1, 0, 2)
        load_d(0)
        load_d(1)
        load_y(1, 2, 4)
        load_sens(0, 1)
        load_sens(1, 1)
        load_tau()

        on_vector = (v_copy, v_copy)
        shared = (v_copy, s_copy)
        keep_clock(4)
        split_words(0, on_vector)
        turn(0)
        for i in (1, 2, 3):
            keep_clock(1)
            split_words(i, on_vector)
            quant_w(i - 1, 0)
            turn(i)
        quant_w(0, 1)
        for g in (0, 1):
            for i in (0, 1, 2):
                stage1(i, 0, (g,))
        quant_w(3, 0)
        stage1(3, 0, (0, 1))
        quant_w(1, 1)
        split_words(4, on_vector)
        turn(4)
        quant_w(2, 1)
        quant_w(3, 1)
        for i in range(4):
            stage1(i, 0, (2, 3))
        split_words(5, shared)
        quant_w(4, 0)
        quant_w(4, 1)
        transpose_w(5)
        weigh(0, 0)
        copy_w(5, 0)
        weigh(1, 0)
        copy_w(5, 1)
        stage1(4, 0)
        split_words(6, shared)
        weigh(2, 0)
        transpose_w(6)
        quant_w(5, 0)
        quant_w(5, 1)
        copy_w(6, 0)
        stage1(5, 0)
        split_words(7, shared)
        quant_w(6, 0)
        copy_w(6, 1)
        weigh(3, 0)
        weigh(4, 0)
        turn(7)
        quant_w(6, 1)
        stage1(6, 0)
        quant_w(7, 0)
        quant_w(7, 1)
        stage1(7, 0)
        interleave(v_copy, z_il[0, 0], z_rows[0, 0], 0, N // 2)
        interleave(s_copy, z_il[0, 0], z_rows[0, 0], N // 2, N)
        weigh(5, 0)
        interleave(s_copy, d_il[0], d_rows[0], 0, F // 2)
        interleave(v_copy, d_il[0], d_rows[0], F // 2, F)
        for i in range(4):
            stage1(i, 1, (0, 1))
        weigh(6, 0)
        weigh(7, 0)
        quant_z(0, 0)
        quant_d(0)
        interleave(s_copy, d_il[1], d_rows[1])
        interleave(s_copy, z_il[1, 0], z_rows[1, 0])
        for i in range(4):
            stage1(i, 1, (2, 3))
            weigh(i, 1)
        interleave(s_copy, z_il[0, 1], z_rows[0, 1])
        quant_d(1)
        quant_z(1, 0)
        nc.vector.tensor_scalar(out=neg_tau[:], in0=tau_raw[:, :, 0], scalar1=-1.0, scalar2=None, op0=ALU.mult)
        for i in (4, 5):
            stage1(i, 1)
            weigh(i, 1)
        stage1(6, 1)
        quant_z(0, 1)
        weigh(6, 1)
        for j in (0, 1):
            stage2(0, j, 0)
            stage2(0, j, 1)
            magnitude(0, j)
        for j in (0, 1):
            threshold(0, j, on_scalar=True)
        stage1(7, 1)
        weigh(7, 1, 0, N // 2)
        weigh(7, 1, N // 2, N)
        interleave(s_copy, z_il[1, 1], z_rows[1, 1], 0, N // 4)
        interleave(v_copy, z_il[1, 1], z_rows[1, 1], N // 4, N // 2)
        interleave(v_copy, z_il[1, 1], z_rows[1, 1], N // 2, N)
        quant_z(1, 1, 0, N // 2)
        quant_z(1, 1, N // 2, N)
        for j in (2, 3):
            stage2(0, j, 0)
            stage2(0, j, 1)
            magnitude(0, j)
            threshold(0, j)
        for j in range(4):
            stage2(1, j, 0)
        for j in range(4):
            stage2(1, j, 1)
            magnitude(1, j)
            threshold(1, j)
